import numpy as np
CORES = [97,105,113,121,225,233,241,249,353,361,369,377,481,489,497,505]
N = 16
PERM = [[0,7],[1,9],[2,15],[3,13],[4,4],[5,0],[6,3],[7,10],[8,2],[9,11],[10,1],[11,6],[12,14],[13,5],[14,12],[15,8]]
def setup_inputs(rng):
    return {"x": rng.standard_normal((N, 128, 16), dtype=np.float32)}
def reference(x):
    y = np.empty_like(x)
    for s, d in PERM:
        y[d] = x[s]
    return {"y": y}

SCRATCH = {
    "stage": ("dram", [128, 16], "float32"),
    "land": ("dram", [128, 16], "float32"),
}
SEMAPHORES = ["loaded", "sent", "arrived", "stored"]

RELAY = {
    0: 98,
    1: 232,
    2: 498,
    5: 234,
    6: 114,
    7: 378,
    8: 496,
    10: 242,
    11: 250,
    13: 360,
    15: 506,
}


def _engines(mask):
    n = 0
    while mask:
        n += mask & 1
        mask >>= 1
    return n


def _send(g, T, topo, src, dst, buf):
    rid, pid = topo.addr(dst, src)
    mask = topo.mask(src, dst)
    g.remote_dma(out_ap=T.land[:], in_ap=buf[:], remote_sem=T.sem.arrived, local_sem=T.sem.sent,
                 pid=pid, routing_id=rid, dma_engine_mask=mask)
    return _engines(mask)


def rank_program(g, core, T, topo):
    cores = T.cores
    perm = T.tables["PERM"]
    rank = T.rank_of(core)

    if rank is None:
        for s, d in perm:
            if s != d and RELAY.get(s) == core:
                g.wait_ge(T.sem.arrived, _engines(topo.mask(cores[s], core)))
                n = _send(g, T, topo, core, cores[d], T.land)
                g.wait_ge(T.sem.sent, n)
        return

    dst = [d for s, d in perm if s == rank][0]
    src = [s for s, d in perm if d == rank][0]

    if dst == rank:
        g.sync.dma_start(T.y[:], T.x[:]).then_inc(T.sem.stored, 16)
        g.sync.wait_ge(T.sem.stored, 16)
        return

    g.sync.dma_start(T.stage[:], T.x[:]).then_inc(T.sem.loaded, 16)
    g.wait_ge(T.sem.loaded, 16)
    n = _send(g, T, topo, core, RELAY.get(rank, cores[dst]), T.stage)

    last = RELAY.get(src, cores[src])
    g.scalar.wait_ge(T.sem.arrived, _engines(topo.mask(last, core)))
    g.scalar.dma_start(T.y[:], T.land[:]).then_inc(T.sem.stored, 16)
    g.scalar.wait_ge(T.sem.stored, 16)

    g.wait_ge(T.sem.sent, n)
